import numpy as np
import ml_dtypes


def mxq(x, axis, fmt="e4m3"):
    dtype, down = {"e4m3": (ml_dtypes.float8_e4m3fn, 7), "e5m2": (ml_dtypes.float8_e5m2, 14)}[fmt]
    v = np.moveaxis(np.asarray(x, np.float32).astype(ml_dtypes.bfloat16).astype(np.float64), axis, -1)
    blocks = v.reshape(v.shape[:-1] + (-1, 32))
    amax = np.abs(blocks).max(-1, keepdims=True)
    byte = np.maximum(np.where(amax > 0, np.frexp(amax)[1] - 1 + 127, 0) - down, 1)
    scale = np.exp2(byte - 127.0)
    codes = (blocks / scale).astype(np.float32).astype(dtype).astype(np.float64)
    return np.moveaxis((codes * scale).reshape(v.shape), -1, axis)


WIDE = False


def mx_kscale(k):
    if not WIDE:
        return np.ones(k)
    levels = np.array([10, -10, 5, -5, 0])
    if k % 512:
        return np.exp2(np.random.permutation(np.resize(levels, k // 32))).repeat(32)
    a = np.empty((k // 512, 16))
    for p in range(k // 512):
        a[p, :8] = np.random.permutation(np.resize(levels, 8))
        for g in range(8):
            far = levels[np.abs(levels - a[p, g]) >= 10]
            a[p, g + 8] = far[np.random.randint(len(far))]
    return np.exp2(a.ravel()).repeat(32)


BF16 = ml_dtypes.bfloat16


def bf(x):
    return np.asarray(x, np.float32).astype(BF16)


def f64(x):
    return np.asarray(x).astype(np.float64)


M, N = 1024, 1536

BETA = 0.9
DELTA = 0.4
KAPPA = 1.0
DECAY = 0.1
LR = 0.75


def inverse_factor(d):
    e = np.random.standard_normal((d, d))
    return np.eye(d) + DELTA * (e + e.T) / np.sqrt(2 * d)


def draw0():
    s, u = mx_kscale(N), mx_kscale(M)
    return {"grad": bf(np.random.standard_normal((M, N)) * s * u[:, None]),
            "b_inv": bf(inverse_factor(N) / s[:, None]),
            "gain": bf(0.5 + np.random.random(N)),
            "vel": bf(0.5 * np.random.standard_normal((M, N)) * u[:, None]),
            "a_inv": bf(inverse_factor(M) / u),
            "w": bf(np.random.standard_normal((M, N)))}


def core(grad, b_inv, gain, vel, a_inv, w):
    gb = mxq(f64(grad), 1, "e4m3") @ mxq(f64(b_inv), 0, "e4m3")
    h = gb * f64(gain) + BETA * f64(vel)
    p = mxq(f64(a_inv), 1, "e4m3") @ mxq(h, 0, "e4m3")
    nu = 1.0 / np.sqrt(1.0 + np.mean(p * p, axis=0) / KAPPA)
    return (1.0 - DECAY) * f64(w) - LR * nu * p


def e4m3fn_bytes(y):
    return np.clip(np.asarray(y, np.float64), -448.0, 448.0).astype(np.float32).astype(ml_dtypes.float8_e4m3fn).view(np.uint8)


def e4m3fn_values(b):
    return np.asarray(b, np.uint8).view(ml_dtypes.float8_e4m3fn).astype(np.float64)


def setup_inputs():
    d = draw0()
    x0 = np.asarray(d['b_inv']).astype(np.float64)
    s = (np.max(np.abs(x0), axis=(1,), keepdims=True) / 448.0).astype(np.float32)
    out = {}
    for k, v in d.items():
        if k == 'b_inv':
            out['b_inv_bytes'] = e4m3fn_bytes(x0 / s.astype(np.float64))
            out['b_inv_scale'] = s
        else:
            out[k] = v
    return out


def reference(grad, b_inv_bytes, b_inv_scale, gain, vel, a_inv, w):
    return core(grad, e4m3fn_values(b_inv_bytes) * b_inv_scale.astype(np.float64), gain, vel, a_inv, w)

@@ -1,0 +1,357 @@
+from contextlib import ExitStack
+
+import concourse.mybir as mybir
+from concourse.masks import make_identity
+
+M, N = 1024, 1536
+FLOPS = 2 * M * N * N + 2 * M * M * N
+
+F32 = mybir.dt.float32
+BF16 = mybir.dt.bfloat16
+U32 = mybir.dt.uint32
+U8 = mybir.dt.uint8
+FP8 = mybir.dt.float8_e4m3fn
+X4 = mybir.dt.float8_e4m3fn_x4
+ALU = mybir.AluOpType
+ACT = mybir.ActivationFunctionType
+
+P = 128
+BW = 512
+GB = {512: 5, 256: 4}
+PB = {512: 3, 256: 4}
+CH = [256] * 5 + [128] * 2
+HEAD = "SSSDSSDDSSSS"
+GE = "SSSSSSSSSSSS"
+AE = "SSSSSSSS"
+AS = [2,2,2,2]
+BE = ["SSSS","SSSS","SSSS","SSSS","SSDD","SSDD","SSDD","SSDD","SSDD","SSDD","SSDD","SSDD"]
+IE = "DDSDSSSSDSSD"
+US = [0,0,1,1,2,2,3,4,5,6,7,7]
+FE = ["SD","SD","SD","SD","SD","SD","SD","SD","SD","SD","SD","SD"]
+CE = ["SS","SS","SS","SS","SS","SS","SS","SS","SS","SS","SS","SD"]
+WE = "DDDDDDDDDDDD"
+BETA, LR, KEEP = 0.9, 0.75, 0.9
+
+
+def tile_kfac_two_sided_step_f4_kernel(
+    tc, grad, b_inv_bytes, b_inv_scale, gain, vel, a_inv, w, out
+):
+    nc = tc.nc
+    grad_v = grad.rearrange("(g p t) k -> g p t k", p=P, t=4)
+    bytes_v = b_inv_bytes.rearrange("(g p t) n -> g p t n", p=P, t=4)
+    scale_v = b_inv_scale.rearrange("(g p t) o -> p g (t o)", p=P, t=4)
+    vel_v = vel.rearrange("(g p t) n -> g p t n", p=P, t=4)
+    a_v = a_inv.rearrange("(p r) k -> p r k", r=8)
+    w_v = w.rearrange("(p r) n -> p r n", r=8)
+    out_v = out.rearrange("(p r) n -> p r n", r=8)
+
+    with ExitStack() as ctx:
+        keep = ctx.enter_context(tc.tile_pool(name="keep", bufs=1))
+        work = ctx.enter_context(tc.tile_pool(name="work", bufs=2))
+        psum = ctx.enter_context(tc.psum_pool(name="psum", bufs=1))
+
+        ident = keep.tile([P, P], F32, name="ident")
+        warm = keep.tile([P, 1], F32, name="warm")
+        make_identity(nc, ident[:])
+        neg_ident = keep.tile([P, P], BF16, name="neg_ident")
+        ctx.enter_context(tc.manual_schedule())
+        nc.vector.tensor_scalar(out=neg_ident[:], in0=ident[:], scalar1=-1.0, scalar2=None, op0=ALU.mult)
+        nc.gpsimd.memset(warm[:], 1.0)
+        nc.scalar.activation(out=warm[:], in_=warm[:], func=ACT.Sqrt)
+
+        c_start = [sum(CH[:c]) for c in range(len(CH))]
+        jt_chunk = [c for c in range(len(CH)) for e in range(CH[c] // P)]
+
+        scale_sb = keep.tile([P, 3, 4], F32, name="scale_sb")
+        nc.sync.dma_start(out=scale_sb[:], in_=scale_v)
+        byte_tiles = {}
+
+        def load_bytes(c0, width):
+            for g in range(3):
+                byte_tile = keep.tile([P, 4, width], U8, name=f"bytes_{c0}_{g}")
+                nc.sync.dma_start(out=byte_tile[:], in_=bytes_v[g][:, :, c0 : c0 + width])
+                for jc in range(c0 // BW, (c0 + width) // BW):
+                    byte_tiles[(jc, g)] = (byte_tile, jc * BW - c0)
+
+        grad_sb = {}
+        load_bytes(0, BW)
+        for g in range(2):
+            grad_sb[g] = work.tile([P, 4, N], BF16, name="raw12", tag="raw12", bufs=2)
+            for x in range(2):
+                nc.sync.dma_start(out=grad_sb[g][:, 2 * x : 2 * x + 2, :], in_=grad_v[g][:, 2 * x : 2 * x + 2, :])
+        gain_sb = keep.tile([P, N], BF16, name="gain_sb")
+        nc.sync.dma_start(out=gain_sb[:], in_=gain.partition_broadcast(P))
+        vel_sb = keep.tile([P, 2, 4, N], BF16, name="vel_sb")
+        for g in range(2):
+            nc.sync.dma_start(out=vel_sb[:, g, :, 0:BW], in_=vel_v[g][:, :, 0:BW])
+        load_bytes(BW, BW)
+        a_sb = keep.tile([P, 8, M], BF16, name="a_sb")
+        for x in range(2):
+            nc.sync.dma_start(out=a_sb[:, 4 * x : 4 * x + 4, :], in_=a_v[:, 4 * x : 4 * x + 4, :])
+        load_bytes(2 * BW, BW)
+        w_sb = {}
+
+        def load_w(x):
+            w_sb[x] = work.tile([P, 8, N // 2], BF16, name="raw12", tag="raw12", bufs=2)
+            nc.sync.dma_start(out=w_sb[x][:], in_=w_v[:, :, x * (N // 2) : (x + 1) * (N // 2)])
+
+        g_codes = keep.tile([P, 3, M], U32, name="g_codes", align_bytes=64)
+        g_scales = keep.tile([P, 3, M], U8, name="g_scales", align_bytes=64)
+        b_codes = keep.tile([P, 3, N], U32, name="b_codes", align_bytes=64)
+        b_scales = keep.tile([P, 3, N], U8, name="b_scales", align_bytes=64)
+        a_codes = keep.tile([P, 2, M], U32, name="a_codes", align_bytes=64)
+        a_scales = keep.tile([P, 2, M], U8, name="a_scales", align_bytes=64)
+
+        def bank(i):
+            return psum.tile([P, 512], F32, name=f"bank{i}")
+
+        planes, grouped = {}, {}
+        unit_width = {}
+
+        def new_grouped(key, width=BW):
+            grouped[key] = work.tile([P, 4 * width], BF16, name=f"grouped{width}", tag=f"grouped{width}", bufs=GB[width], align_bytes=64)
+
+        def widen(c0, width, g, t, eng):
+            if (c0, g) not in planes:
+                planes[(c0, g)] = work.tile([P, 4, width], BF16, name=f"planes{width}", tag=f"planes{width}", bufs=PB[width])
+            byte_tile, b0 = byte_tiles[(c0 // BW, g)]
+            b0 = b0 + c0 % BW
+            src = byte_tile[:, t, b0 : b0 + width].bitcast(FP8)
+            if eng == "S":
+                nc.scalar.activation(out=planes[(c0, g)][:, t, :], in_=src, func=ACT.Copy, scale=scale_sb[:, g, t : t + 1])
+            else:
+                nc.vector.tensor_scalar(out=planes[(c0, g)][:, t, :], in0=src, scalar1=scale_sb[:, g, t : t + 1], scalar2=None, op0=ALU.mult)
+
+        def interleave(c0, width, g, eng):
+            key = ("b", c0, g)
+            new_grouped(key, width)
+            dst = grouped[key][:].rearrange("p (n t) -> p n t", t=4)
+            src = planes[(c0, g)][:].rearrange("p t n -> p n t")
+            if eng == "S":
+                nc.scalar.copy(out=dst, in_=src)
+            else:
+                nc.vector.tensor_copy(out=dst, in_=src)
+
+        def quant_b(c0, width, g):
+            c = slice(c0, c0 + width)
+            nc.vector.quantize_mx(out=b_codes[:, g, c].bitcast(X4), scales=b_scales[:, g, c], in_=grouped[("b", c0, g)][:])
+
+        def turn(src_rows, key, c, x, b, eng):
+            tb = bank(b)
+            for i in range(2):
+                words = src_rows[:, 2 * x + i, :].bitcast(F32)
+                for u in range(2):
+                    nc.tensor.transpose(tb[:, 128 * (2 * i + u) : 128 * (2 * i + u + 1)], words[:, 256 * c + u : 256 * (c + 1) : 2], ident[:])
+            if key not in grouped:
+                new_grouped(key)
+            dst = grouped[key][:].bitcast(F32)[:, 512 * x : 512 * (x + 1)].rearrange("p (i m u) -> p i m u", i=2, u=2)
+            src = tb[:].rearrange("p (i u m) -> p i m u", i=2, u=2)
+            if eng == "S":
+                nc.scalar.copy(out=dst, in_=src)
+            else:
+                nc.vector.tensor_copy(out=dst, in_=src)
+
+        def quant_g(g, c):
+            cols = slice(512 * g, 512 * (g + 1))
+            nc.vector.quantize_mx(out=g_codes[:, c, cols].bitcast(X4), scales=g_scales[:, c, cols], in_=grouped[("g", g, c)][:])
+
+        def quant_a(h, c):
+            cols = slice(512 * h, 512 * (h + 1))
+            nc.vector.quantize_mx(out=a_codes[:, c, cols].bitcast(X4), scales=a_scales[:, c, cols], in_=grouped[("a", h, c)][:])
+
+        gb, hh, h_codes, h_scales, prod, grp_h = {}, {}, {}, {}, {}, {}
+
+        def mx1(s):
+            c, g = divmod(s, 2)
+            width = CH[c]
+            per = 512 // width
+            J = slice(c_start[c], c_start[c] + width)
+            for th in range(4 // per):
+                gb[(s, th)] = bank(th)
+                for i in range(per):
+                    m = slice(512 * g + 128 * (per * th + i), 512 * g + 128 * (per * th + i + 1))
+                    for k in range(3):
+                        nc.tensor.matmul_mx(
+                            out=gb[(s, th)][:, width * i : width * (i + 1)],
+                            lhsT=g_codes[:, k, m].bitcast(X4), lhsT_scale=g_scales[:, k, m],
+                            rhs=b_codes[:, k, J].bitcast(X4), rhs_scale=b_scales[:, k, J],
+                            start=(k == 0), stop=(k == 2))
+
+        def op1(s):
+            c, g = divmod(s, 2)
+            width = CH[c]
+            per = 512 // width
+            J = slice(c_start[c], c_start[c] + width)
+            prod[s] = work.tile([P, 4, width], F32, name="prod", tag="prod", bufs=2)
+            gn = gain_sb[:, J].unsqueeze(1).to_broadcast([P, per, width])
+            for th in range(4 // per):
+                nc.vector.tensor_tensor(out=prod[s][:, per * th : per * (th + 1), :], in0=gb[(s, th)][:].rearrange("p (t n) -> p t n", t=per), in1=gn, op=ALU.mult)
+
+        def op2(s):
+            c, g = divmod(s, 2)
+            width = CH[c]
+            J = slice(c_start[c], c_start[c] + width)
+            if c not in grp_h:
+                grp_h[c] = work.tile([P, 2, 4 * width], BF16, name="grp_h", tag="grp_h", bufs=2, align_bytes=64)
+            nc.vector.scalar_tensor_tensor(
+                out=grp_h[c][:, g, :].rearrange("p (n t) -> p n t", t=4),
+                in0=vel_sb[:, g, :, J].rearrange("p t n -> p n t"), scalar=BETA,
+                in1=prod[s][:].rearrange("p t n -> p n t"), op0=ALU.mult, op1=ALU.add)
+
+        def quant_h(c):
+            width = CH[c]
+            h_codes[c] = work.tile([P, 2, width], U32, name="h_codes", tag="h_codes", bufs=3, align_bytes=64)
+            h_scales[c] = work.tile([P, 2, width], U8, name="h_scales", tag="h_scales", bufs=3, align_bytes=64)
+            nc.vector.quantize_mx(out=h_codes[c][:].rearrange("p g n -> p (g n)").bitcast(X4), scales=h_scales[c][:].rearrange("p g n -> p (g n)"), in_=grp_h[c][:].rearrange("p g n -> p (g n)"))
+
+        pt, stat, scaled, turned, res = {}, {}, {}, {}, {}
+
+        def mx2(jt):
+            c = jt_chunk[jt]
+            e = jt - c_start[c] // P
+            m = slice(128 * e, 128 * (e + 1))
+            for half in range(2):
+                pt[(jt, half)] = bank(2 + 2 * (jt % 2) + half)
+                cols = slice(512 * half, 512 * (half + 1))
+                for g in range(2):
+                    nc.tensor.matmul_mx(
+                        out=pt[(jt, half)][:],
+                        lhsT=h_codes[c][:, g, m].bitcast(X4), lhsT_scale=h_scales[c][:, g, m],
+                        rhs=a_codes[:, g, cols].bitcast(X4), rhs_scale=a_scales[:, g, cols],
+                        start=(g == 0), stop=(g == 1))
+
+        def square(jt):
+            stat[jt] = [work.tile([P, 1], F32, name=f"st{i}", tag=f"st{i}", bufs=3) for i in range(5)]
+            for half in range(2):
+                junk = work.tile([P, 512], BF16, name="junk", tag="junk", bufs=2)
+                nc.scalar.activation(out=junk[:], in_=pt[(jt, half)][:], func=ACT.Square, accum_out=stat[jt][half][:])
+
+        def root(jt):
+            s0, s1, base, rt, nu = stat[jt]
+            k = (KEEP * KEEP if WE[jt] == "P" else 1.0) / (LR * LR)
+            nc.scalar.activation(out=base[:], in_=s1[:], func=ACT.Copy, scale=k / M, bias=k)
+            nc.scalar.activation(out=rt[:], in_=s0[:], func=ACT.Sqrt, scale=k / M, bias=base[:])
+
+        def recip(jt):
+            nc.vector.reciprocal(out=stat[jt][4][:], in_=stat[jt][3][:])
+
+        def scale_out(jt):
+            scaled[jt] = work.tile([P, M], F32, name="scaled", tag="scaled", bufs=3)
+            for half in range(2):
+                cols = slice(512 * half, 512 * (half + 1))
+                if CE[jt][half] == "S":
+                    nc.scalar.activation(out=scaled[jt][:, cols], in_=pt[(jt, half)][:], func=ACT.Copy, scale=stat[jt][4][:])
+                else:
+                    nc.vector.tensor_scalar(out=scaled[jt][:, cols], in0=pt[(jt, half)][:], scalar1=stat[jt][4][:], scalar2=None, op0=ALU.mult)
+
+        def t2(jt):
+            x, jj = divmod(128 * jt, N // 2)
+            for half in range(2):
+                turned[(jt, half)] = bank(6 + half)
+                r0 = 4 * half
+                if WE[jt] == "P":
+                    nc.tensor.matmul(
+                        out=turned[(jt, half)][:].rearrange("p (r n) -> p r n", r=4), lhsT=neg_ident[:],
+                        rhs=w_sb[x][:, r0 : r0 + 4, jj : jj + 128], start=True, stop=False)
+                for i in range(4):
+                    r = r0 + i
+                    nc.tensor.matmul(
+                        out=turned[(jt, half)][:, 128 * i : 128 * (i + 1)], lhsT=scaled[jt][:, 128 * r : 128 * (r + 1)],
+                        rhs=ident[:], start=(WE[jt] == "D"), stop=(WE[jt] == "D" or i == 3), is_transpose=True)
+
+        def finish(jt):
+            c = jt_chunk[jt]
+            e = jt - c_start[c] // P
+            if c not in res:
+                res[c] = work.tile([P, 8, CH[c]], F32, name="res", tag="res", bufs=2)
+            for half in range(2):
+                r = slice(4 * half, 4 * half + 4)
+                dst = res[c][:, r, 128 * e : 128 * (e + 1)]
+                src = turned[(jt, half)][:].rearrange("p (r n) -> p r n", r=4)
+                if WE[jt] == "D":
+                    x, jj = divmod(128 * jt, N // 2)
+                    nc.vector.scalar_tensor_tensor(out=dst, in0=w_sb[x][:, r, jj : jj + 128], scalar=KEEP, in1=src, op0=ALU.mult, op1=ALU.subtract)
+                elif FE[jt][half] == "S":
+                    nc.scalar.activation(out=dst, in_=src, func=ACT.Copy, scale=-KEEP)
+                else:
+                    nc.vector.tensor_scalar(out=dst, in0=src, scalar1=-KEEP, scalar2=None, op0=ALU.mult)
+                if 128 * (e + 1) == CH[c]:
+                    nc.sync.dma_start(out=out_v[:, r, c_start[c] : c_start[c] + CH[c]], in_=res[c][:, r, :])
+
+        for t in range(4):
+            widen(0, BW, 0, t, HEAD[t])
+        interleave(0, BW, 0, "D")
+        for g in (1, 2):
+            for t in range(4):
+                widen(0, BW, g, t, HEAD[4 * g + t])
+        interleave(0, BW, 1, "D")
+        quant_b(0, BW, 0)
+        interleave(0, BW, 2, "D")
+        quant_b(0, BW, 1)
+
+        def turn_grad(g, x):
+            for c in range(3):
+                turn(grad_sb[g], ("g", g, c), c, x, 2 + (3 * x + c) % 6, GE[6 * g + 3 * x + c])
+                if x == 1 and c > 0:
+                    quant_g(g, c - 1)
+            if x == 1:
+                quant_g(g, 2)
+
+        turn_grad(0, 0)
+        quant_b(0, BW, 2)
+        turn_grad(0, 1)
+        turn_grad(1, 0)
+        turn_grad(1, 1)
+        load_w(0)
+        for g in range(2):
+            nc.sync.dma_start(out=vel_sb[:, g, :, BW:N], in_=vel_v[g][:, :, BW:N])
+        load_w(1)
+
+        units = [(512 + 256 * (u // 3), u % 3) for u in range(12)]
+        nstep = 2 * len(CH)
+        n_jt = N // P
+        enter = [2 * jt_chunk[jt] + 3 + jt - c_start[jt_chunk[jt]] // P for jt in range(n_jt)]
+
+        def jts(s):
+            return [jt for jt in range(n_jt) if enter[jt] == s]
+
+        for s in range(enter[-1] + 3):
+            for jt in jts(s - 2):
+                t2(jt)
+            for q in range(4):
+                if AS[q] == s:
+                    for x in range(2):
+                        h, c = divmod(q, 2)
+                        turn(a_sb[:, 4 * h : 4 * h + 4, :], ("a", h, c), c, x, 2 + 2 * c + x, AE[2 * q + x])
+            if 0 <= s - 1 < nstep:
+                op1(s - 1)
+            for q in range(4):
+                if AS[q] == s - 1:
+                    quant_a(*divmod(q, 2))
+            if s < nstep:
+                mx1(s)
+            for jt in jts(s):
+                mx2(jt)
+            for u in range(12):
+                if US[u] == s - 1:
+                    interleave(units[u][0], 256, units[u][1], IE[u])
+            for u in range(12):
+                if US[u] == s - 2:
+                    quant_b(units[u][0], 256, units[u][1])
+            for u in range(12):
+                if US[u] == s:
+                    for t in range(4):
+                        widen(units[u][0], 256, units[u][1], t, BE[u][t])
+            if 0 <= s - 1 < nstep:
+                op2(s - 1)
+            for jt in jts(s - 1):
+                recip(jt)
+            for jt in jts(s - 2):
+                finish(jt)
+            for jt in jts(s - 1):
+                scale_out(jt)
+            for jt in jts(s):
+                square(jt)
+                root(jt)
+            if 0 <= s - 1 < nstep and (s - 1) % 2 == 1:
+                quant_h((s - 1) // 2)

@@ -17,19 +17,21 @@ ACT = mybir.ActivationFunctionType
 
 P = 128
 BW = 512
-GB = {512: 5, 256: 4}
-PB = {512: 3, 256: 4}
-CH = [256] * 5 + [128] * 2
-HEAD = "SSSDSSDDSSSS"
-GE = "SSSSSSSSSSSS"
+GBB = 6
+PBB = 3
+GE = "SDSSSSSDSDSD"
 AE = "SSSSSSSS"
-AS = [2,2,2,2]
-BE = ["SSSS","SSSS","SSSS","SSSS","SSDD","SSDD","SSDD","SSDD","SSDD","SSDD","SSDD","SSDD"]
-IE = "DDSDSSSSDSSD"
-US = [0,0,1,1,2,2,3,4,5,6,7,7]
-FE = ["SD","SD","SD","SD","SD","SD","SD","SD","SD","SD","SD","SD"]
-CE = ["SS","SS","SS","SS","SS","SS","SS","SS","SS","SS","SS","SD"]
-WE = "DDDDDDDDDDDD"
+AS = [0,0,1,1]
+BE = ["DSDS","SSDS","SSSS","DDDS","SSDD","DSSS","SSSS","SDDD","DSSD"]
+IE = "DDDDSSDSS"
+US = [1,2,4]
+CE = ["SS","SS","SS","DS","SS","DS","DS","SS","SS","SS","SD","SD"]
+LO = [["r"], ["g", 0], ["g", 1], ["v", 0, 512], ["a"]]
+VR = 512
+VB = 3
+M0 = False
+HO = ["W","w0","i0","w1","q0","i1","w3","w2","w4","q1","i4","i3","i2","t00","q2","t01","q3","q4","W","Q0","t10","t11","m","w5","Q1","i5","S","q5"]
+SG = "DDS"
 BETA, LR, KEEP = 0.9, 0.75, 0.9
 
 
@@ -53,42 +55,41 @@ def tile_kfac_two_sided_step_f4_kernel(
         ident = keep.tile([P, P], F32, name="ident")
         warm = keep.tile([P, 1], F32, name="warm")
         make_identity(nc, ident[:])
-        neg_ident = keep.tile([P, P], BF16, name="neg_ident")
         ctx.enter_context(tc.manual_schedule())
-        nc.vector.tensor_scalar(out=neg_ident[:], in0=ident[:], scalar1=-1.0, scalar2=None, op0=ALU.mult)
         nc.gpsimd.memset(warm[:], 1.0)
         nc.scalar.activation(out=warm[:], in_=warm[:], func=ACT.Sqrt)
-
-        c_start = [sum(CH[:c]) for c in range(len(CH))]
-        jt_chunk = [c for c in range(len(CH)) for e in range(CH[c] // P)]
 
         scale_sb = keep.tile([P, 3, 4], F32, name="scale_sb")
         nc.sync.dma_start(out=scale_sb[:], in_=scale_v)
         byte_tiles = {}
-
-        def load_bytes(c0, width):
-            for g in range(3):
-                byte_tile = keep.tile([P, 4, width], U8, name=f"bytes_{c0}_{g}")
-                nc.sync.dma_start(out=byte_tile[:], in_=bytes_v[g][:, :, c0 : c0 + width])
-                for jc in range(c0 // BW, (c0 + width) // BW):
-                    byte_tiles[(jc, g)] = (byte_tile, jc * BW - c0)
+        for g in range(3):
+            for x in range(2):
+                byte_tile = keep.tile([P, 2, N], U8, name=f"bytes_{g}_{x}")
+                nc.sync.dma_start(out=byte_tile[:], in_=bytes_v[g][:, 2 * x : 2 * x + 2, :])
+                byte_tiles[(g, x)] = byte_tile
 
         grad_sb = {}
-        load_bytes(0, BW)
-        for g in range(2):
-            grad_sb[g] = work.tile([P, 4, N], BF16, name="raw12", tag="raw12", bufs=2)
-            for x in range(2):
-                nc.sync.dma_start(out=grad_sb[g][:, 2 * x : 2 * x + 2, :], in_=grad_v[g][:, 2 * x : 2 * x + 2, :])
+        gain_row = keep.tile([P, N], BF16, name="gain_row")
+        ones = keep.tile([P, 512], BF16, name="ones")
+        nc.gpsimd.memset(ones[:], 1.0)
+        nc.gpsimd.memset(gain_row[:], 0.0)
         gain_sb = keep.tile([P, N], BF16, name="gain_sb")
-        nc.sync.dma_start(out=gain_sb[:], in_=gain.partition_broadcast(P))
         vel_sb = keep.tile([P, 2, 4, N], BF16, name="vel_sb")
-        for g in range(2):
-            nc.sync.dma_start(out=vel_sb[:, g, :, 0:BW], in_=vel_v[g][:, :, 0:BW])
-        load_bytes(BW, BW)
         a_sb = keep.tile([P, 8, M], BF16, name="a_sb")
-        for x in range(2):
-            nc.sync.dma_start(out=a_sb[:, 4 * x : 4 * x + 4, :], in_=a_v[:, 4 * x : 4 * x + 4, :])
-        load_bytes(2 * BW, BW)
+        for tok in LO:
+            if tok[0] == "r":
+                nc.sync.dma_start(out=gain_row[0:1, :], in_=gain.rearrange("(o n) -> o n", o=1))
+            elif tok[0] == "g":
+                g = tok[1]
+                grad_sb[g] = work.tile([P, 4, N], BF16, name="raw12", tag="raw12", bufs=2)
+                for x in range(2):
+                    nc.sync.dma_start(out=grad_sb[g][:, 2 * x : 2 * x + 2, :], in_=grad_v[g][:, 2 * x : 2 * x + 2, :])
+            elif tok[0] == "v":
+                for g in range(2):
+                    nc.sync.dma_start(out=vel_sb[:, g, :, tok[1] : tok[2]], in_=vel_v[g][:, :, tok[1] : tok[2]])
+            elif tok[0] == "a":
+                for x in range(2):
+                    nc.sync.dma_start(out=a_sb[:, 4 * x : 4 * x + 4, :], in_=a_v[:, 4 * x : 4 * x + 4, :])
         w_sb = {}
 
         def load_w(x):
@@ -106,35 +107,42 @@ def tile_kfac_two_sided_step_f4_kernel(
             return psum.tile([P, 512], F32, name=f"bank{i}")
 
         planes, grouped = {}, {}
-        unit_width = {}
 
-        def new_grouped(key, width=BW):
-            grouped[key] = work.tile([P, 4 * width], BF16, name=f"grouped{width}", tag=f"grouped{width}", bufs=GB[width], align_bytes=64)
+        def new_grouped(key):
+            grouped[key] = work.tile([P, 4 * BW], BF16, name="grouped", tag="grouped", bufs=GBB, align_bytes=64)
 
-        def widen(c0, width, g, t, eng):
-            if (c0, g) not in planes:
-                planes[(c0, g)] = work.tile([P, 4, width], BF16, name=f"planes{width}", tag=f"planes{width}", bufs=PB[width])
-            byte_tile, b0 = byte_tiles[(c0 // BW, g)]
-            b0 = b0 + c0 % BW
-            src = byte_tile[:, t, b0 : b0 + width].bitcast(FP8)
-            if eng == "S":
-                nc.scalar.activation(out=planes[(c0, g)][:, t, :], in_=src, func=ACT.Copy, scale=scale_sb[:, g, t : t + 1])
+        def widen(u, t):
+            jc, g = divmod(u, 3)
+            if u not in planes:
+                planes[u] = work.tile([P, 4, BW], BF16, name="planes", tag="planes", bufs=PBB)
+            src = byte_tiles[(g, t // 2)][:, t % 2, jc * BW : (jc + 1) * BW].bitcast(FP8)
+            if BE[u][t] == "S":
+                nc.scalar.activation(out=planes[u][:, t, :], in_=src, func=ACT.Copy, scale=scale_sb[:, g, t : t + 1])
             else:
-                nc.vector.tensor_scalar(out=planes[(c0, g)][:, t, :], in0=src, scalar1=scale_sb[:, g, t : t + 1], scalar2=None, op0=ALU.mult)
+                nc.vector.tensor_scalar(out=planes[u][:, t, :], in0=src, scalar1=scale_sb[:, g, t : t + 1], scalar2=None, op0=ALU.mult)
 
-        def interleave(c0, width, g, eng):
-            key = ("b", c0, g)
-            new_grouped(key, width)
-            dst = grouped[key][:].rearrange("p (n t) -> p n t", t=4)
-            src = planes[(c0, g)][:].rearrange("p t n -> p n t")
-            if eng == "S":
+        def interleave(u):
+            new_grouped(("b", u))
+            dst = grouped[("b", u)][:].rearrange("p (n t) -> p n t", t=4)
+            src = planes[u][:].rearrange("p t n -> p n t")
+            if IE[u] == "S":
                 nc.scalar.copy(out=dst, in_=src)
             else:
                 nc.vector.tensor_copy(out=dst, in_=src)
 
-        def quant_b(c0, width, g):
-            c = slice(c0, c0 + width)
-            nc.vector.quantize_mx(out=b_codes[:, g, c].bitcast(X4), scales=b_scales[:, g, c], in_=grouped[("b", c0, g)][:])
+        def quant_b(u):
+            jc, g = divmod(u, 3)
+            c = slice(jc * BW, (jc + 1) * BW)
+            nc.vector.quantize_mx(out=b_codes[:, g, c].bitcast(X4), scales=b_scales[:, g, c], in_=grouped[("b", u)][:])
+
+        def spread_gain(x):
+            gp = bank(2 + x)
+            cols = slice(512 * x, 512 * (x + 1))
+            nc.tensor.matmul(out=gp[:], lhsT=ones[:, 0:P], rhs=gain_row[:, cols], start=True, stop=True)
+            if SG[x] == "S":
+                nc.scalar.copy(out=gain_sb[:, cols], in_=gp[:])
+            else:
+                nc.vector.tensor_copy(out=gain_sb[:, cols], in_=gp[:])
 
         def turn(src_rows, key, c, x, b, eng):
             tb = bank(b)
@@ -159,64 +167,58 @@ def tile_kfac_two_sided_step_f4_kernel(
             cols = slice(512 * h, 512 * (h + 1))
             nc.vector.quantize_mx(out=a_codes[:, c, cols].bitcast(X4), scales=a_scales[:, c, cols], in_=grouped[("a", h, c)][:])
 
-        gb, hh, h_codes, h_scales, prod, grp_h = {}, {}, {}, {}, {}, {}
+        gb, h_codes, h_scales, prod, grp_h = {}, {}, {}, {}, {}
 
-        def mx1(s):
-            c, g = divmod(s, 2)
-            width = CH[c]
-            per = 512 // width
-            J = slice(c_start[c], c_start[c] + width)
-            for th in range(4 // per):
-                gb[(s, th)] = bank(th)
-                for i in range(per):
-                    m = slice(512 * g + 128 * (per * th + i), 512 * g + 128 * (per * th + i + 1))
+        def mx1(j, g):
+            J = slice(P * j, P * (j + 1))
+            if True:
+                gb[(j, g)] = bank(g)
+                for i in range(4):
+                    m = slice(512 * g + 128 * i, 512 * g + 128 * (i + 1))
                     for k in range(3):
                         nc.tensor.matmul_mx(
-                            out=gb[(s, th)][:, width * i : width * (i + 1)],
+                            out=gb[(j, g)][:, 128 * i : 128 * (i + 1)],
                             lhsT=g_codes[:, k, m].bitcast(X4), lhsT_scale=g_scales[:, k, m],
                             rhs=b_codes[:, k, J].bitcast(X4), rhs_scale=b_scales[:, k, J],
                             start=(k == 0), stop=(k == 2))
 
-        def op1(s):
-            c, g = divmod(s, 2)
-            width = CH[c]
-            per = 512 // width
-            J = slice(c_start[c], c_start[c] + width)
-            prod[s] = work.tile([P, 4, width], F32, name="prod", tag="prod", bufs=2)
-            gn = gain_sb[:, J].unsqueeze(1).to_broadcast([P, per, width])
-            for th in range(4 // per):
-                nc.vector.tensor_tensor(out=prod[s][:, per * th : per * (th + 1), :], in0=gb[(s, th)][:].rearrange("p (t n) -> p t n", t=per), in1=gn, op=ALU.mult)
+        def op1(j, g):
+            gn = gain_sb[:, P * j : P * (j + 1)].unsqueeze(2).to_broadcast([P, P, 4])
+            if True:
+                prod[(j, g)] = work.tile([P, P, 4], F32, name="prod", tag="prod", bufs=3)
+                nc.vector.tensor_tensor(out=prod[(j, g)][:], in0=gb[(j, g)][:].rearrange("p (t n) -> p n t", t=4), in1=gn, op=ALU.mult)
 
-        def op2(s):
-            c, g = divmod(s, 2)
-            width = CH[c]
-            J = slice(c_start[c], c_start[c] + width)
-            if c not in grp_h:
-                grp_h[c] = work.tile([P, 2, 4 * width], BF16, name="grp_h", tag="grp_h", bufs=2, align_bytes=64)
-            nc.vector.scalar_tensor_tensor(
-                out=grp_h[c][:, g, :].rearrange("p (n t) -> p n t", t=4),
-                in0=vel_sb[:, g, :, J].rearrange("p t n -> p n t"), scalar=BETA,
-                in1=prod[s][:].rearrange("p t n -> p n t"), op0=ALU.mult, op1=ALU.add)
+        vg = {}
 
-        def quant_h(c):
-            width = CH[c]
-            h_codes[c] = work.tile([P, 2, width], U32, name="h_codes", tag="h_codes", bufs=3, align_bytes=64)
-            h_scales[c] = work.tile([P, 2, width], U8, name="h_scales", tag="h_scales", bufs=3, align_bytes=64)
-            nc.vector.quantize_mx(out=h_codes[c][:].rearrange("p g n -> p (g n)").bitcast(X4), scales=h_scales[c][:].rearrange("p g n -> p (g n)"), in_=grp_h[c][:].rearrange("p g n -> p (g n)"))
+        def vint(j):
+            for g in range(2):
+                vg[(j, g)] = work.tile([P, P, 4], BF16, name=f"vg{g}", tag=f"vg{g}", bufs=VB)
+                nc.gpsimd.tensor_scalar(out=vg[(j, g)][:], in0=vel_sb[:, g, :, P * j : P * (j + 1)].rearrange("p t n -> p n t"), scalar1=1.0, scalar2=0.0, op0=ALU.mult, op1=ALU.add)
+
+        def op2(j, g):
+            if g == 0:
+                grp_h[j] = work.tile([P, 2, 4 * P], BF16, name="grp_h", tag="grp_h", bufs=2, align_bytes=64)
+            if True:
+                nc.vector.scalar_tensor_tensor(
+                    out=grp_h[j][:, g, :].rearrange("p (n t) -> p n t", t=4),
+                    in0=vg[(j, g)][:], scalar=BETA,
+                    in1=prod[(j, g)][:], op0=ALU.mult, op1=ALU.add)
+
+        def quant_h(j):
+            h_codes[j] = work.tile([P, 2, P], U32, name="h_codes", tag="h_codes", bufs=3, align_bytes=64)
+            h_scales[j] = work.tile([P, 2, P], U8, name="h_scales", tag="h_scales", bufs=3, align_bytes=64)
+            nc.vector.quantize_mx(out=h_codes[j][:].rearrange("p g n -> p (g n)").bitcast(X4), scales=h_scales[j][:].rearrange("p g n -> p (g n)"), in_=grp_h[j][:].rearrange("p g n -> p (g n)"))
 
         pt, stat, scaled, turned, res = {}, {}, {}, {}, {}
 
         def mx2(jt):
-            c = jt_chunk[jt]
-            e = jt - c_start[c] // P
-            m = slice(128 * e, 128 * (e + 1))
             for half in range(2):
                 pt[(jt, half)] = bank(2 + 2 * (jt % 2) + half)
                 cols = slice(512 * half, 512 * (half + 1))
                 for g in range(2):
                     nc.tensor.matmul_mx(
                         out=pt[(jt, half)][:],
-                        lhsT=h_codes[c][:, g, m].bitcast(X4), lhsT_scale=h_scales[c][:, g, m],
+                        lhsT=h_codes[jt][:, g, :].bitcast(X4), lhsT_scale=h_scales[jt][:, g, :],
                         rhs=a_codes[:, g, cols].bitcast(X4), rhs_scale=a_scales[:, g, cols],
                         start=(g == 0), stop=(g == 1))
 
@@ -228,7 +230,7 @@ def tile_kfac_two_sided_step_f4_kernel(
 
         def root(jt):
             s0, s1, base, rt, nu = stat[jt]
-            k = (KEEP * KEEP if WE[jt] == "P" else 1.0) / (LR * LR)
+            k = 1.0 / (LR * LR)
             nc.scalar.activation(out=base[:], in_=s1[:], func=ACT.Copy, scale=k / M, bias=k)
             nc.scalar.activation(out=rt[:], in_=s0[:], func=ACT.Sqrt, scale=k / M, bias=base[:])
 
@@ -244,114 +246,121 @@ def tile_kfac_two_sided_step_f4_kernel(
                 else:
                     nc.vector.tensor_scalar(out=scaled[jt][:, cols], in0=pt[(jt, half)][:], scalar1=stat[jt][4][:], scalar2=None, op0=ALU.mult)
 
-        def t2(jt):
-            x, jj = divmod(128 * jt, N // 2)
-            for half in range(2):
+        def t2(jt, half):
+            if True:
                 turned[(jt, half)] = bank(6 + half)
                 r0 = 4 * half
-                if WE[jt] == "P":
-                    nc.tensor.matmul(
-                        out=turned[(jt, half)][:].rearrange("p (r n) -> p r n", r=4), lhsT=neg_ident[:],
-                        rhs=w_sb[x][:, r0 : r0 + 4, jj : jj + 128], start=True, stop=False)
                 for i in range(4):
                     r = r0 + i
-                    nc.tensor.matmul(
-                        out=turned[(jt, half)][:, 128 * i : 128 * (i + 1)], lhsT=scaled[jt][:, 128 * r : 128 * (r + 1)],
-                        rhs=ident[:], start=(WE[jt] == "D"), stop=(WE[jt] == "D" or i == 3), is_transpose=True)
+                    nc.tensor.transpose(turned[(jt, half)][:, 128 * i : 128 * (i + 1)], scaled[jt][:, 128 * r : 128 * (r + 1)], ident[:])
 
-        def finish(jt):
-            c = jt_chunk[jt]
-            e = jt - c_start[c] // P
-            if c not in res:
-                res[c] = work.tile([P, 8, CH[c]], F32, name="res", tag="res", bufs=2)
-            for half in range(2):
+        def finish(jt, half):
+            c, e = divmod(jt, 2)
+            if e == 0 and half == 0:
+                res[c] = work.tile([P, 8, 2 * P], F32, name="res", tag="res", bufs=2)
+            x, jj = divmod(P * jt, N // 2)
+            if True:
                 r = slice(4 * half, 4 * half + 4)
-                dst = res[c][:, r, 128 * e : 128 * (e + 1)]
-                src = turned[(jt, half)][:].rearrange("p (r n) -> p r n", r=4)
-                if WE[jt] == "D":
-                    x, jj = divmod(128 * jt, N // 2)
-                    nc.vector.scalar_tensor_tensor(out=dst, in0=w_sb[x][:, r, jj : jj + 128], scalar=KEEP, in1=src, op0=ALU.mult, op1=ALU.subtract)
-                elif FE[jt][half] == "S":
-                    nc.scalar.activation(out=dst, in_=src, func=ACT.Copy, scale=-KEEP)
-                else:
-                    nc.vector.tensor_scalar(out=dst, in0=src, scalar1=-KEEP, scalar2=None, op0=ALU.mult)
-                if 128 * (e + 1) == CH[c]:
-                    nc.sync.dma_start(out=out_v[:, r, c_start[c] : c_start[c] + CH[c]], in_=res[c][:, r, :])
+                nc.vector.scalar_tensor_tensor(
+                    out=res[c][:, r, P * e : P * (e + 1)], in0=w_sb[x][:, r, jj : jj + P], scalar=KEEP,
+                    in1=turned[(jt, half)][:].rearrange("p (r n) -> p r n", r=4), op0=ALU.mult, op1=ALU.subtract)
+                if e == 1 or jt == 10:
+                    cols = slice(P * jt, P * (jt + 1)) if jt >= 10 else slice(2 * P * c, 2 * P * (c + 1))
+                    rc = slice(P * e, P * (e + 1)) if jt >= 10 else slice(0, 2 * P)
+                    nc.sync.dma_start(out=out_v[:, r, cols], in_=res[c][:, r, rc])
 
-        for t in range(4):
-            widen(0, BW, 0, t, HEAD[t])
-        interleave(0, BW, 0, "D")
-        for g in (1, 2):
+        def warm_on(src):
+            warm_bank = bank(0)
+            nc.tensor.matmul(out=warm_bank[:], lhsT=ones[:, 0:P], rhs=src, start=True, stop=True)
+
+        def wid(u):
             for t in range(4):
-                widen(0, BW, g, t, HEAD[4 * g + t])
-        interleave(0, BW, 1, "D")
-        quant_b(0, BW, 0)
-        interleave(0, BW, 2, "D")
-        quant_b(0, BW, 1)
+                widen(u, t)
 
         def turn_grad(g, x):
             for c in range(3):
                 turn(grad_sb[g], ("g", g, c), c, x, 2 + (3 * x + c) % 6, GE[6 * g + 3 * x + c])
-                if x == 1 and c > 0:
-                    quant_g(g, c - 1)
-            if x == 1:
-                quant_g(g, 2)
 
-        turn_grad(0, 0)
-        quant_b(0, BW, 2)
-        turn_grad(0, 1)
-        turn_grad(1, 0)
-        turn_grad(1, 1)
+        def head(tok):
+            kind, arg = tok[0], tok[1:]
+            if kind == "w":
+                wid(int(arg))
+                if int(arg) == 2:
+                    for t in range(4):
+                        warm_on(planes[2][:, t, :])
+            elif kind == "i":
+                interleave(int(arg))
+            elif kind == "q":
+                quant_b(int(arg))
+            elif kind == "t":
+                turn_grad(int(arg[0]), int(arg[1]))
+            elif kind == "Q":
+                for c in range(3):
+                    quant_g(int(arg), c)
+            elif kind == "S":
+                for x in range(3):
+                    spread_gain(x)
+            elif kind == "m":
+                mx1(0, 0)
+            elif kind == "W":
+                for i in range(2):
+                    warm_on(ones[:])
+
+        for tok in HO:
+            head(tok)
         load_w(0)
-        for g in range(2):
-            nc.sync.dma_start(out=vel_sb[:, g, :, BW:N], in_=vel_v[g][:, :, BW:N])
+        if VR < N:
+            for g in range(2):
+                nc.sync.dma_start(out=vel_sb[:, g, :, VR:N], in_=vel_v[g][:, :, VR:N])
         load_w(1)
 
-        units = [(512 + 256 * (u // 3), u % 3) for u in range(12)]
-        nstep = 2 * len(CH)
         n_jt = N // P
-        enter = [2 * jt_chunk[jt] + 3 + jt - c_start[jt_chunk[jt]] // P for jt in range(n_jt)]
-
-        def jts(s):
-            return [jt for jt in range(n_jt) if enter[jt] == s]
-
-        for s in range(enter[-1] + 3):
-            for jt in jts(s - 2):
-                t2(jt)
+        for j in range(VB):
+            vint(j)
+        for s in range(n_jt + 4):
+            if 0 <= s - 4:
+                t2(s - 4, 0)
+                t2(s - 4, 1)
+            if 0 <= s - 1 < n_jt:
+                op1(s - 1, 0)
+                op1(s - 1, 1)
+            if 0 < s < n_jt:
+                mx1(s, 0)
+            if s < n_jt:
+                mx1(s, 1)
+            if 0 <= s - 3 < n_jt:
+                recip(s - 3)
+            if 0 <= s - 1 < n_jt:
+                op2(s - 1, 0)
+                op2(s - 1, 1)
+                if s - 1 + VB < n_jt:
+                    vint(s - 1 + VB)
+            if 0 <= s - 4:
+                finish(s - 4, 0)
+                finish(s - 4, 1)
+            for q in range(4):
+                if AS[q] == s - 1:
+                    quant_a(*divmod(q, 2))
+            if 0 <= s - 2 < n_jt:
+                mx2(s - 2)
+            for u in (6, 7, 8):
+                if US[u - 6] == s - 2:
+                    interleave(u)
+                if US[u - 6] == s - 3:
+                    quant_b(u)
+                for i in range(2):
+                    if US[u - 6] == s - i:
+                        widen(u, 2 * i)
+                        widen(u, 2 * i + 1)
             for q in range(4):
                 if AS[q] == s:
                     for x in range(2):
                         h, c = divmod(q, 2)
-                        turn(a_sb[:, 4 * h : 4 * h + 4, :], ("a", h, c), c, x, 2 + 2 * c + x, AE[2 * q + x])
-            if 0 <= s - 1 < nstep:
-                op1(s - 1)
-            for q in range(4):
-                if AS[q] == s - 1:
-                    quant_a(*divmod(q, 2))
-            if s < nstep:
-                mx1(s)
-            for jt in jts(s):
-                mx2(jt)
-            for u in range(12):
-                if US[u] == s - 1:
-                    interleave(units[u][0], 256, units[u][1], IE[u])
-            for u in range(12):
-                if US[u] == s - 2:
-                    quant_b(units[u][0], 256, units[u][1])
-            for u in range(12):
-                if US[u] == s:
-                    for t in range(4):
-                        widen(units[u][0], 256, units[u][1], t, BE[u][t])
-            if 0 <= s - 1 < nstep:
-                op2(s - 1)
-            for jt in jts(s - 1):
-                recip(jt)
-            for jt in jts(s - 2):
-                finish(jt)
-            for jt in jts(s - 1):
-                scale_out(jt)
-            for jt in jts(s):
-                square(jt)
-                root(jt)
-            if 0 <= s - 1 < nstep and (s - 1) % 2 == 1:
-                quant_h((s - 1) // 2)
+                        turn(a_sb[:, 4 * h : 4 * h + 4, :], ("a", h, c), c, x, 2 + (2 * q + x) % 6, AE[2 * q + x])
+            if 0 <= s - 3 < n_jt:
+                scale_out(s - 3)
+            if 0 <= s - 2 < n_jt:
+                square(s - 2)
+                root(s - 2)
+            if 0 <= s - 1 < n_jt:
+                quant_h(s - 1)

from contextlib import ExitStack

import concourse.mybir as mybir
from concourse.masks import make_identity

M, N = 1024, 1536
FLOPS = 2 * M * N * N + 2 * M * M * N

F32 = mybir.dt.float32
BF16 = mybir.dt.bfloat16
U32 = mybir.dt.uint32
U8 = mybir.dt.uint8
FP8 = mybir.dt.float8_e4m3fn
X4 = mybir.dt.float8_e4m3fn_x4
ALU = mybir.AluOpType
ACT = mybir.ActivationFunctionType

P = 128
BW = 512
GBB = 6
PBB = 3
GE = "SDSSSSSDSDSD"
AE = "SSSSSSSS"
AS = [0,0,1,1]
BE = ["DSDS","SSDS","SSSS","DDDS","SSDD","DSSS","SSSS","SDDD","DSSD"]
IE = "DDDDSSDSS"
US = [1,2,4]
CE = ["SS","SS","SS","DS","SS","DS","DS","SS","SS","SS","SD","SD"]
LO = [["r"], ["g", 0], ["g", 1], ["v", 0, 512], ["a"]]
VR = 512
VB = 3
M0 = False
HO = ["W","w0","i0","w1","q0","i1","w3","w2","w4","q1","i4","i3","i2","t00","q2","t01","q3","q4","W","Q0","t10","t11","m","w5","Q1","i5","S","q5"]
SG = "DDS"
BETA, LR, KEEP = 0.9, 0.75, 0.9


def tile_kfac_two_sided_step_f4_kernel(
    tc, grad, b_inv_bytes, b_inv_scale, gain, vel, a_inv, w, out
):
    nc = tc.nc
    grad_v = grad.rearrange("(g p t) k -> g p t k", p=P, t=4)
    bytes_v = b_inv_bytes.rearrange("(g p t) n -> g p t n", p=P, t=4)
    scale_v = b_inv_scale.rearrange("(g p t) o -> p g (t o)", p=P, t=4)
    vel_v = vel.rearrange("(g p t) n -> g p t n", p=P, t=4)
    a_v = a_inv.rearrange("(p r) k -> p r k", r=8)
    w_v = w.rearrange("(p r) n -> p r n", r=8)
    out_v = out.rearrange("(p r) n -> p r n", r=8)

    with ExitStack() as ctx:
        keep = ctx.enter_context(tc.tile_pool(name="keep", bufs=1))
        work = ctx.enter_context(tc.tile_pool(name="work", bufs=2))
        psum = ctx.enter_context(tc.psum_pool(name="psum", bufs=1))

        ident = keep.tile([P, P], F32, name="ident")
        warm = keep.tile([P, 1], F32, name="warm")
        make_identity(nc, ident[:])
        ctx.enter_context(tc.manual_schedule())
        nc.gpsimd.memset(warm[:], 1.0)
        nc.scalar.activation(out=warm[:], in_=warm[:], func=ACT.Sqrt)

        scale_sb = keep.tile([P, 3, 4], F32, name="scale_sb")
        nc.sync.dma_start(out=scale_sb[:], in_=scale_v)
        byte_tiles = {}
        for g in range(3):
            for x in range(2):
                byte_tile = keep.tile([P, 2, N], U8, name=f"bytes_{g}_{x}")
                nc.sync.dma_start(out=byte_tile[:], in_=bytes_v[g][:, 2 * x : 2 * x + 2, :])
                byte_tiles[(g, x)] = byte_tile

        grad_sb = {}
        gain_row = keep.tile([P, N], BF16, name="gain_row")
        ones = keep.tile([P, 512], BF16, name="ones")
        nc.gpsimd.memset(ones[:], 1.0)
        nc.gpsimd.memset(gain_row[:], 0.0)
        gain_sb = keep.tile([P, N], BF16, name="gain_sb")
        vel_sb = keep.tile([P, 2, 4, N], BF16, name="vel_sb")
        a_sb = keep.tile([P, 8, M], BF16, name="a_sb")
        for tok in LO:
            if tok[0] == "r":
                nc.sync.dma_start(out=gain_row[0:1, :], in_=gain.rearrange("(o n) -> o n", o=1))
            elif tok[0] == "g":
                g = tok[1]
                grad_sb[g] = work.tile([P, 4, N], BF16, name="raw12", tag="raw12", bufs=2)
                for x in range(2):
                    nc.sync.dma_start(out=grad_sb[g][:, 2 * x : 2 * x + 2, :], in_=grad_v[g][:, 2 * x : 2 * x + 2, :])
            elif tok[0] == "v":
                for g in range(2):
                    nc.sync.dma_start(out=vel_sb[:, g, :, tok[1] : tok[2]], in_=vel_v[g][:, :, tok[1] : tok[2]])
            elif tok[0] == "a":
                for x in range(2):
                    nc.sync.dma_start(out=a_sb[:, 4 * x : 4 * x + 4, :], in_=a_v[:, 4 * x : 4 * x + 4, :])
        w_sb = {}

        def load_w(x):
            w_sb[x] = work.tile([P, 8, N // 2], BF16, name="raw12", tag="raw12", bufs=2)
            nc.sync.dma_start(out=w_sb[x][:], in_=w_v[:, :, x * (N // 2) : (x + 1) * (N // 2)])

        g_codes = keep.tile([P, 3, M], U32, name="g_codes", align_bytes=64)
        g_scales = keep.tile([P, 3, M], U8, name="g_scales", align_bytes=64)
        b_codes = keep.tile([P, 3, N], U32, name="b_codes", align_bytes=64)
        b_scales = keep.tile([P, 3, N], U8, name="b_scales", align_bytes=64)
        a_codes = keep.tile([P, 2, M], U32, name="a_codes", align_bytes=64)
        a_scales = keep.tile([P, 2, M], U8, name="a_scales", align_bytes=64)

        def bank(i):
            return psum.tile([P, 512], F32, name=f"bank{i}")

        planes, grouped = {}, {}

        def new_grouped(key):
            grouped[key] = work.tile([P, 4 * BW], BF16, name="grouped", tag="grouped", bufs=GBB, align_bytes=64)

        def widen(u, t):
            jc, g = divmod(u, 3)
            if u not in planes:
                planes[u] = work.tile([P, 4, BW], BF16, name="planes", tag="planes", bufs=PBB)
            src = byte_tiles[(g, t // 2)][:, t % 2, jc * BW : (jc + 1) * BW].bitcast(FP8)
            if BE[u][t] == "S":
                nc.scalar.activation(out=planes[u][:, t, :], in_=src, func=ACT.Copy, scale=scale_sb[:, g, t : t + 1])
            else:
                nc.vector.tensor_scalar(out=planes[u][:, t, :], in0=src, scalar1=scale_sb[:, g, t : t + 1], scalar2=None, op0=ALU.mult)

        def interleave(u):
            new_grouped(("b", u))
            dst = grouped[("b", u)][:].rearrange("p (n t) -> p n t", t=4)
            src = planes[u][:].rearrange("p t n -> p n t")
            if IE[u] == "S":
                nc.scalar.copy(out=dst, in_=src)
            else:
                nc.vector.tensor_copy(out=dst, in_=src)

        def quant_b(u):
            jc, g = divmod(u, 3)
            c = slice(jc * BW, (jc + 1) * BW)
            nc.vector.quantize_mx(out=b_codes[:, g, c].bitcast(X4), scales=b_scales[:, g, c], in_=grouped[("b", u)][:])

        def spread_gain(x):
            gp = bank(2 + x)
            cols = slice(512 * x, 512 * (x + 1))
            nc.tensor.matmul(out=gp[:], lhsT=ones[:, 0:P], rhs=gain_row[:, cols], start=True, stop=True)
            if SG[x] == "S":
                nc.scalar.copy(out=gain_sb[:, cols], in_=gp[:])
            else:
                nc.vector.tensor_copy(out=gain_sb[:, cols], in_=gp[:])

        def turn(src_rows, key, c, x, b, eng):
            tb = bank(b)
            for i in range(2):
                words = src_rows[:, 2 * x + i, :].bitcast(F32)
                for u in range(2):
                    nc.tensor.transpose(tb[:, 128 * (2 * i + u) : 128 * (2 * i + u + 1)], words[:, 256 * c + u : 256 * (c + 1) : 2], ident[:])
            if key not in grouped:
                new_grouped(key)
            dst = grouped[key][:].bitcast(F32)[:, 512 * x : 512 * (x + 1)].rearrange("p (i m u) -> p i m u", i=2, u=2)
            src = tb[:].rearrange("p (i u m) -> p i m u", i=2, u=2)
            if eng == "S":
                nc.scalar.copy(out=dst, in_=src)
            else:
                nc.vector.tensor_copy(out=dst, in_=src)

        def quant_g(g, c):
            cols = slice(512 * g, 512 * (g + 1))
            nc.vector.quantize_mx(out=g_codes[:, c, cols].bitcast(X4), scales=g_scales[:, c, cols], in_=grouped[("g", g, c)][:])

        def quant_a(h, c):
            cols = slice(512 * h, 512 * (h + 1))
            nc.vector.quantize_mx(out=a_codes[:, c, cols].bitcast(X4), scales=a_scales[:, c, cols], in_=grouped[("a", h, c)][:])

        gb, h_codes, h_scales, prod, grp_h = {}, {}, {}, {}, {}

        def mx1(j, g):
            J = slice(P * j, P * (j + 1))
            if True:
                gb[(j, g)] = bank(g)
                for i in range(4):
                    m = slice(512 * g + 128 * i, 512 * g + 128 * (i + 1))
                    for k in range(3):
                        nc.tensor.matmul_mx(
                            out=gb[(j, g)][:, 128 * i : 128 * (i + 1)],
                            lhsT=g_codes[:, k, m].bitcast(X4), lhsT_scale=g_scales[:, k, m],
                            rhs=b_codes[:, k, J].bitcast(X4), rhs_scale=b_scales[:, k, J],
                            start=(k == 0), stop=(k == 2))

        def op1(j, g):
            gn = gain_sb[:, P * j : P * (j + 1)].unsqueeze(2).to_broadcast([P, P, 4])
            if True:
                prod[(j, g)] = work.tile([P, P, 4], F32, name="prod", tag="prod", bufs=3)
                nc.vector.tensor_tensor(out=prod[(j, g)][:], in0=gb[(j, g)][:].rearrange("p (t n) -> p n t", t=4), in1=gn, op=ALU.mult)

        vg = {}

        def vint(j):
            for g in range(2):
                vg[(j, g)] = work.tile([P, P, 4], BF16, name=f"vg{g}", tag=f"vg{g}", bufs=VB)
                nc.gpsimd.tensor_scalar(out=vg[(j, g)][:], in0=vel_sb[:, g, :, P * j : P * (j + 1)].rearrange("p t n -> p n t"), scalar1=1.0, scalar2=0.0, op0=ALU.mult, op1=ALU.add)

        def op2(j, g):
            if g == 0:
                grp_h[j] = work.tile([P, 2, 4 * P], BF16, name="grp_h", tag="grp_h", bufs=2, align_bytes=64)
            if True:
                nc.vector.scalar_tensor_tensor(
                    out=grp_h[j][:, g, :].rearrange("p (n t) -> p n t", t=4),
                    in0=vg[(j, g)][:], scalar=BETA,
                    in1=prod[(j, g)][:], op0=ALU.mult, op1=ALU.add)

        def quant_h(j):
            h_codes[j] = work.tile([P, 2, P], U32, name="h_codes", tag="h_codes", bufs=3, align_bytes=64)
            h_scales[j] = work.tile([P, 2, P], U8, name="h_scales", tag="h_scales", bufs=3, align_bytes=64)
            nc.vector.quantize_mx(out=h_codes[j][:].rearrange("p g n -> p (g n)").bitcast(X4), scales=h_scales[j][:].rearrange("p g n -> p (g n)"), in_=grp_h[j][:].rearrange("p g n -> p (g n)"))

        pt, stat, scaled, turned, res = {}, {}, {}, {}, {}

        def mx2(jt):
            for half in range(2):
                pt[(jt, half)] = bank(2 + 2 * (jt % 2) + half)
                cols = slice(512 * half, 512 * (half + 1))
                for g in range(2):
                    nc.tensor.matmul_mx(
                        out=pt[(jt, half)][:],
                        lhsT=h_codes[jt][:, g, :].bitcast(X4), lhsT_scale=h_scales[jt][:, g, :],
                        rhs=a_codes[:, g, cols].bitcast(X4), rhs_scale=a_scales[:, g, cols],
                        start=(g == 0), stop=(g == 1))

        def square(jt):
            stat[jt] = [work.tile([P, 1], F32, name=f"st{i}", tag=f"st{i}", bufs=3) for i in range(5)]
            for half in range(2):
                junk = work.tile([P, 512], BF16, name="junk", tag="junk", bufs=2)
                nc.scalar.activation(out=junk[:], in_=pt[(jt, half)][:], func=ACT.Square, accum_out=stat[jt][half][:])

        def root(jt):
            s0, s1, base, rt, nu = stat[jt]
            k = 1.0 / (LR * LR)
            nc.scalar.activation(out=base[:], in_=s1[:], func=ACT.Copy, scale=k / M, bias=k)
            nc.scalar.activation(out=rt[:], in_=s0[:], func=ACT.Sqrt, scale=k / M, bias=base[:])

        def recip(jt):
            nc.vector.reciprocal(out=stat[jt][4][:], in_=stat[jt][3][:])

        def scale_out(jt):
            scaled[jt] = work.tile([P, M], F32, name="scaled", tag="scaled", bufs=3)
            for half in range(2):
                cols = slice(512 * half, 512 * (half + 1))
                if CE[jt][half] == "S":
                    nc.scalar.activation(out=scaled[jt][:, cols], in_=pt[(jt, half)][:], func=ACT.Copy, scale=stat[jt][4][:])
                else:
                    nc.vector.tensor_scalar(out=scaled[jt][:, cols], in0=pt[(jt, half)][:], scalar1=stat[jt][4][:], scalar2=None, op0=ALU.mult)

        def t2(jt, half):
            if True:
                turned[(jt, half)] = bank(6 + half)
                r0 = 4 * half
                for i in range(4):
                    r = r0 + i
                    nc.tensor.transpose(turned[(jt, half)][:, 128 * i : 128 * (i + 1)], scaled[jt][:, 128 * r : 128 * (r + 1)], ident[:])

        def finish(jt, half):
            c, e = divmod(jt, 2)
            if e == 0 and half == 0:
                res[c] = work.tile([P, 8, 2 * P], F32, name="res", tag="res", bufs=2)
            x, jj = divmod(P * jt, N // 2)
            if True:
                r = slice(4 * half, 4 * half + 4)
                nc.vector.scalar_tensor_tensor(
                    out=res[c][:, r, P * e : P * (e + 1)], in0=w_sb[x][:, r, jj : jj + P], scalar=KEEP,
                    in1=turned[(jt, half)][:].rearrange("p (r n) -> p r n", r=4), op0=ALU.mult, op1=ALU.subtract)
                if e == 1 or jt == 10:
                    cols = slice(P * jt, P * (jt + 1)) if jt >= 10 else slice(2 * P * c, 2 * P * (c + 1))
                    rc = slice(P * e, P * (e + 1)) if jt >= 10 else slice(0, 2 * P)
                    nc.sync.dma_start(out=out_v[:, r, cols], in_=res[c][:, r, rc])

        def warm_on(src):
            warm_bank = bank(0)
            nc.tensor.matmul(out=warm_bank[:], lhsT=ones[:, 0:P], rhs=src, start=True, stop=True)

        def wid(u):
            for t in range(4):
                widen(u, t)

        def turn_grad(g, x):
            for c in range(3):
                turn(grad_sb[g], ("g", g, c), c, x, 2 + (3 * x + c) % 6, GE[6 * g + 3 * x + c])

        def head(tok):
            kind, arg = tok[0], tok[1:]
            if kind == "w":
                wid(int(arg))
                if int(arg) == 2:
                    for t in range(4):
                        warm_on(planes[2][:, t, :])
            elif kind == "i":
                interleave(int(arg))
            elif kind == "q":
                quant_b(int(arg))
            elif kind == "t":
                turn_grad(int(arg[0]), int(arg[1]))
            elif kind == "Q":
                for c in range(3):
                    quant_g(int(arg), c)
            elif kind == "S":
                for x in range(3):
                    spread_gain(x)
            elif kind == "m":
                mx1(0, 0)
            elif kind == "W":
                for i in range(2):
                    warm_on(ones[:])

        for tok in HO:
            head(tok)
        load_w(0)
        if VR < N:
            for g in range(2):
                nc.sync.dma_start(out=vel_sb[:, g, :, VR:N], in_=vel_v[g][:, :, VR:N])
        load_w(1)

        n_jt = N // P
        for j in range(VB):
            vint(j)
        for s in range(n_jt + 4):
            if 0 <= s - 4:
                t2(s - 4, 0)
                t2(s - 4, 1)
            if 0 <= s - 1 < n_jt:
                op1(s - 1, 0)
                op1(s - 1, 1)
            if 0 < s < n_jt:
                mx1(s, 0)
            if s < n_jt:
                mx1(s, 1)
            if 0 <= s - 3 < n_jt:
                recip(s - 3)
            if 0 <= s - 1 < n_jt:
                op2(s - 1, 0)
                op2(s - 1, 1)
                if s - 1 + VB < n_jt:
                    vint(s - 1 + VB)
            if 0 <= s - 4:
                finish(s - 4, 0)
                finish(s - 4, 1)
            for q in range(4):
                if AS[q] == s - 1:
                    quant_a(*divmod(q, 2))
            if 0 <= s - 2 < n_jt:
                mx2(s - 2)
            for u in (6, 7, 8):
                if US[u - 6] == s - 2:
                    interleave(u)
                if US[u - 6] == s - 3:
                    quant_b(u)
                for i in range(2):
                    if US[u - 6] == s - i:
                        widen(u, 2 * i)
                        widen(u, 2 * i + 1)
            for q in range(4):
                if AS[q] == s:
                    for x in range(2):
                        h, c = divmod(q, 2)
                        turn(a_sb[:, 4 * h : 4 * h + 4, :], ("a", h, c), c, x, 2 + (2 * q + x) % 6, AE[2 * q + x])
            if 0 <= s - 3 < n_jt:
                scale_out(s - 3)
            if 0 <= s - 2 < n_jt:
                square(s - 2)
                root(s - 2)
            if 0 <= s - 1 < n_jt:
                quant_h(s - 1)
